import numpy as np
import ml_dtypes


def mxq(x, axis, fmt="e4m3"):
    dtype, down = {"e4m3": (ml_dtypes.float8_e4m3fn, 7), "e5m2": (ml_dtypes.float8_e5m2, 14)}[fmt]
    v = np.moveaxis(np.asarray(x, np.float32).astype(ml_dtypes.bfloat16).astype(np.float64), axis, -1)
    blocks = v.reshape(v.shape[:-1] + (-1, 32))
    amax = np.abs(blocks).max(-1, keepdims=True)
    byte = np.maximum(np.where(amax > 0, np.frexp(amax)[1] - 1 + 127, 0) - down, 1)
    scale = np.exp2(byte - 127.0)
    codes = (blocks / scale).astype(np.float32).astype(dtype).astype(np.float64)
    return np.moveaxis((codes * scale).reshape(v.shape), -1, axis)


WIDE = False


def mx_kscale(k):
    if not WIDE:
        return np.ones(k)
    levels = np.array([30, -30])
    if k % 512:
        return np.exp2(np.random.permutation(np.resize(levels, k // 32))).repeat(32)
    a = np.empty((k // 512, 16))
    for p in range(k // 512):
        a[p, :8] = np.random.permutation(np.resize(levels, 8))
        for g in range(8):
            far = levels[np.abs(levels - a[p, g]) >= 10]
            a[p, g + 8] = far[np.random.randint(len(far))]
    return np.exp2(a.ravel()).repeat(32)


def f64(x):
    return np.asarray(x).astype(np.float64)


def striped(idx):
    return np.tile(np.asarray(idx).reshape(-1, 16).T, (8, 1)).astype(np.uint16)


def unstriped(offs):
    return offs[:16].T.reshape(-1).astype(np.int64)


E2M1 = np.array([0.0, 0.5, 1.0, 1.5, 2.0, 3.0, 4.0, 6.0, -0.0, -0.5, -1.0, -1.5, -2.0, -3.0, -4.0, -6.0])


def pack_weight(w, fmt):
    k, n = w.shape
    w = f64(np.asarray(w, np.float32).astype(ml_dtypes.bfloat16)).reshape(k // 32, 32, n)
    amax = np.abs(w).max(1)
    if fmt in ("e4m3", "e5m2"):
        byte = np.frexp(amax)[1] - 1 + 127 - (7 if fmt == "e4m3" else 14)
    else:
        mant, ex = np.frexp(amax / 6.0)
        byte = np.where(mant > 0.5, ex, ex - 1) + 127
    byte = np.clip(np.where(amax > 0, byte, 1), 1, 254)
    scaled = (w * np.exp2(127.0 - byte)[:, None, :]).reshape(k, n).astype(np.float32)
    by_word = np.ascontiguousarray(scaled.reshape(k // 512, 128, 4, n).transpose(0, 1, 3, 2))
    if fmt in ("e4m3", "e5m2"):
        words = by_word.astype(ml_dtypes.float8_e4m3fn if fmt == "e4m3" else ml_dtypes.float8_e5m2).view(np.uint8)
    else:
        c = by_word.astype(ml_dtypes.float4_e2m1fn).view(np.uint8) & 0xF
        words = (c[..., 0::2] | (c[..., 1::2] << 4)).reshape(k // 512, 128, 2 * n)
    return np.ascontiguousarray(words), np.ascontiguousarray(byte.astype(np.uint8).reshape(k // 512, 16, n))


def unpack_weight(words, scales, fmt):
    g, _, n = scales.shape
    words = np.ascontiguousarray(words).reshape(g, 128, n, -1)
    if fmt in ("e4m3", "e5m2"):
        vals = words.view(ml_dtypes.float8_e4m3fn if fmt == "e4m3" else ml_dtypes.float8_e5m2).astype(np.float64)
    else:
        nib = np.empty((g, 128, n, 4), np.uint8)
        nib[..., 0::2] = words & 0xF
        nib[..., 1::2] = words >> 4
        vals = E2M1[nib]
    vals = vals * np.repeat(np.exp2(scales.astype(np.float64) - 127.0), 8, axis=1)[..., None]
    return vals.transpose(0, 1, 3, 2).reshape(g * 512, n)


def e4m3fn_bytes(y):
    return np.clip(np.asarray(y, np.float64), -448.0, 448.0).astype(np.float32).astype(ml_dtypes.float8_e4m3fn).view(np.uint8)


def e4m3fn_values(b):
    return np.asarray(b, np.uint8).view(ml_dtypes.float8_e4m3fn).astype(np.float64)


K, T, J, R, F, Z, V, D, N = 512, 1024, 256, 512, 512, 1024, 1024, 512, 256


def setup_inputs():
    n = np.random.standard_normal
    idx = np.random.permutation(T)[:J]
    idx2 = np.random.permutation(Z)[:J]
    idx3 = np.random.permutation(V)[:J]
    idx4 = np.random.permutation(D)[:J]
    fk = mx_kscale(K)
    ff = mx_kscale(F)
    fr = mx_kscale(R)
    xtp = pack_weight(n((K, T)) / fk[:, None], "e2m1")
    xop = pack_weight(n((F, Z)) / ff[:, None], "e5m2")
    wp = pack_weight(n((K, R)) * 1 / np.sqrt(K) * fk[:, None] * fr, "e5m2")
    w0p = pack_weight(n((F, R)) * 1 / np.sqrt(F) * ff[:, None] * fr, "e4m3")
    wbp = pack_weight(n((R, N)) * 1 / np.sqrt(R) / fr[:, None], "e4m3")
    return {
        "xt_words": xtp[0],
        "xt_scales": xtp[1],
        "xo_words": xop[0],
        "xo_scales": xop[1],
        "w_words": wp[0],
        "w_scales": wp[1],
        "w0_words": w0p[0],
        "w0_scales": w0p[1],
        "wb_words": wbp[0],
        "wb_scales": wbp[1],
        "ca": e4m3fn_bytes(60.0 * n((N, V))),
        "cb": e4m3fn_bytes(60.0 * n((N, D))),
        "sa": (np.random.uniform(0.004, 0.012, (N, 1))).astype(np.float32),
        "sb": (np.random.uniform(0.004, 0.012, (N, 1))).astype(np.float32),
        "offs": striped(idx),
        "offs2": striped(idx2),
        "offs3": striped(idx3),
        "offs4": striped(idx4),
    }


def reference(xt_words, xt_scales, xo_words, xo_scales, w_words, w_scales, w0_words, w0_scales, wb_words, wb_scales, ca, cb, sa, sb, offs, offs2, offs3, offs4):
    idx = unstriped(offs)
    idx2 = unstriped(offs2)
    idx3 = unstriped(offs3)
    idx4 = unstriped(offs4)
    xtu = unpack_weight(xt_words, xt_scales, "e2m1")
    xou = unpack_weight(xo_words, xo_scales, "e5m2")
    wu = unpack_weight(w_words, w_scales, "e5m2")
    w0u = unpack_weight(w0_words, w0_scales, "e4m3")
    wbu = unpack_weight(wb_words, wb_scales, "e4m3")
    xtidxg = xtu[:, idx]
    xoidx2g = xou[:, idx2]
    a = wu.T @ xtidxg + w0u.T @ xoidx2g
    hid = np.maximum(a, 0.0)
    hidq = mxq(hid, 0, "e5m2")
    p = wbu.T @ hidq
    g1 = e4m3fn_values(ca)[:, idx3] * f64(sa)
    g2 = e4m3fn_values(cb)[:, idx4] * f64(sb)
    y = p * g1 + g2
    return y

@@ -1,0 +1,167 @@
+from contextlib import ExitStack
+
+import concourse.mybir as mybir
+from concourse.masks import make_identity
+
+K, T, J, R, F, Z, V, D, N = 512, 1024, 256, 512, 512, 1024, 1024, 512, 256
+FLOPS = 2 * K * R * J + 2 * F * R * J + 2 * R * N * J
+
+F32 = mybir.dt.float32
+BF16 = mybir.dt.bfloat16
+I32 = mybir.dt.int32
+U32 = mybir.dt.uint32
+U16 = mybir.dt.uint16
+U8 = mybir.dt.uint8
+FP8 = mybir.dt.float8_e4m3fn
+E4M3X4 = mybir.dt.float8_e4m3fn_x4
+E5M2X4 = mybir.dt.float8_e5m2_x4
+E2M1X4 = mybir.dt.float4_e2m1fn_x4
+ACT = mybir.ActivationFunctionType
+ALU = mybir.AluOpType
+
+P = 128
+HALVES = 2
+QUADS = 4
+
+
+def words_of(dram):
+    return dram[0].rearrange("p c b -> p (c b)").bitcast(I32)
+
+
+def load_scale_rows(queue, plane, scales):
+    for q in range(QUADS):
+        queue.dma_start(plane[32 * q : 32 * q + 4, :].bitcast(I32), scales[0, 4 * q : 4 * q + 4, :].bitcast(I32))
+
+
+def load_scale_pairs(queue, staged, col, scales):
+    width = scales.shape[2]
+    rows = scales[0].rearrange("(s q r) c -> q r s c", s=2, q=2)
+    for q in range(2):
+        queue.dma_start(staged[32 * q : 32 * q + 4, :, col : col + width].bitcast(I32), rows[q].bitcast(I32))
+
+
+def tile_list_gainandshift_kernel(tc, xt_words, xt_scales, xo_words, xo_scales, w_words, w_scales, w0_words, w0_scales,
+                                       wb_words, wb_scales, ca, cb, sa, sb, offs, offs2, offs3, offs4, out):
+    nc = tc.nc
+    with ExitStack() as ctx:
+        pool = ctx.enter_context(tc.tile_pool(name="held", bufs=1))
+        psum = ctx.enter_context(tc.psum_pool(name="psum", bufs=1))
+
+        lst_t = pool.tile([P, J // 16], U16, name="lst_t")
+        lst_o = pool.tile([P, J // 16], U16, name="lst_o")
+        lst_a = pool.tile([P, J // 16], U16, name="lst_a")
+        lst_b = pool.tile([P, J // 16], U16, name="lst_b")
+        xt_w = pool.tile([P, T], U16, name="xt_w", align_bytes=64)
+        xt_s = pool.tile([P, T], U8, name="xt_s", align_bytes=64)
+        xo_w = pool.tile([P, Z], U32, name="xo_w", align_bytes=64)
+        xo_s = pool.tile([P, Z], U8, name="xo_s", align_bytes=64)
+        w_w = pool.tile([P, R], U32, name="w_w", align_bytes=64)
+        w0_w = pool.tile([P, R], U32, name="w0_w", align_bytes=64)
+        wb_w = pool.tile([P, N], U32, name="wb_w", align_bytes=64)
+        w_s = pool.tile([P, 2, R], U8, name="w_s", align_bytes=64)
+        w0_s = pool.tile([P, 2, R], U8, name="w0_s", align_bytes=64)
+        wb_s = pool.tile([P, N], U8, name="wb_s", align_bytes=64)
+        ca_t = [pool.tile([P, V], U8, name="ca_t%d" % h) for h in range(HALVES)]
+        cb_t = [pool.tile([P, D], U8, name="cb_t%d" % h) for h in range(HALVES)]
+        sa_t = pool.tile([P, HALVES], F32, name="sa_t")
+        sb_t = pool.tile([P, HALVES], F32, name="sb_t")
+        ident = pool.tile([P, P], F32, name="ident", align_bytes=64)
+
+        nc.vector.memset(xt_s[:].bitcast(I32), 0)
+        nc.vector.memset(w_s[0:64].bitcast(I32), 0)
+        nc.vector.memset(xo_s[:].bitcast(I32), 0)
+        nc.vector.memset(w0_s[0:64].bitcast(I32), 0)
+        nc.vector.memset(wb_s[:].bitcast(I32), 0)
+
+        nc.gpsimd.dma_start(xo_w[:].bitcast(I32), words_of(xo_words))
+        nc.gpsimd.dma_start(w_w[:].bitcast(I32), words_of(w_words))
+        nc.gpsimd.dma_start(w0_w[:].bitcast(I32), words_of(w0_words))
+        make_identity(nc, ident[:])
+
+        nc.sync.dma_start(lst_t[:], offs)
+        nc.sync.dma_start(xt_w[:].bitcast(I32), xt_words[0].bitcast(I32))
+        load_scale_rows(nc.sync, xt_s, xt_scales)
+        load_scale_pairs(nc.sync, w_s, 0, w_scales)
+        nc.sync.dma_start(lst_o[:], offs2)
+        load_scale_rows(nc.sync, xo_s, xo_scales)
+        load_scale_pairs(nc.sync, w0_s, 0, w0_scales)
+        nc.sync.dma_start(lst_a[:], offs3)
+        for h in range(HALVES):
+            nc.sync.dma_start(ca_t[h][:], ca[h * P : (h + 1) * P, :])
+        nc.sync.dma_start(lst_b[:], offs4)
+        for h in range(HALVES):
+            nc.sync.dma_start(cb_t[h][:], cb[h * P : (h + 1) * P, :])
+        nc.sync.dma_start(wb_w[:].bitcast(I32), words_of(wb_words))
+        with nc.allow_non_contiguous_dma(reason="one step a partition and half"):
+            nc.sync.dma_start(sa_t[:], sa.rearrange("(h p) o -> p (h o)", p=P))
+            nc.sync.dma_start(sb_t[:], sb.rearrange("(h p) o -> p (h o)", p=P))
+        load_scale_rows(nc.sync, wb_s, wb_scales)
+
+        gt_w = pool.tile([P, J], U16, name="gt_w", align_bytes=64)
+        gt_s = pool.tile([P, J], U8, name="gt_s", align_bytes=64)
+        go_w = pool.tile([P, J], U32, name="go_w", align_bytes=64)
+        go_s = [pool.tile([P, P], U8, name="go_s%d" % h, align_bytes=64) for h in range(HALVES)]
+        nc.vector.tensor_copy(gt_w[:], xt_w[:].indirect(lst_t[:]))
+        nc.vector.tensor_copy(gt_s[:], xt_s[:].indirect(lst_t[:]))
+        nc.vector.tensor_copy(w_s[64:128, 0, :].bitcast(I32), w_s[0:64, 1, :].bitcast(I32))
+        nc.vector.tensor_copy(go_w[:], xo_w[:].indirect(lst_o[:]))
+        for h in range(HALVES):
+            nc.vector.tensor_copy(go_s[h][:], xo_s[:].indirect(lst_o[:, 8 * h : 8 * (h + 1)]))
+
+        nc.vector.tensor_copy(w0_s[64:128, 0, :].bitcast(I32), w0_s[0:64, 1, :].bitcast(I32))
+
+        acc = [psum.tile([P, R], F32, name="acc%d" % h) for h in range(HALVES)]
+        for h in range(HALVES):
+            js = slice(h * P, (h + 1) * P)
+            nc.tensor.matmul_mx(out=acc[h][:], lhsT=gt_w[:, js].bitcast(E2M1X4), lhsT_scale=gt_s[:, js],
+                                rhs=w_w[:].bitcast(E5M2X4), rhs_scale=w_s[:, 0, :], start=True, stop=False)
+        for h in range(HALVES):
+            js = slice(h * P, (h + 1) * P)
+            nc.tensor.matmul_mx(out=acc[h][:], lhsT=go_w[:, js].bitcast(E5M2X4), lhsT_scale=go_s[h][:],
+                                rhs=w0_w[:].bitcast(E4M3X4), rhs_scale=w0_s[:, 0, :], start=False, stop=True)
+
+        ga = [pool.tile([P, J], U8, name="ga%d" % h) for h in range(HALVES)]
+        gb = [pool.tile([P, J], U8, name="gb%d" % h) for h in range(HALVES)]
+        for h in range(HALVES):
+            nc.vector.tensor_copy(ga[h][:], ca_t[h][:].indirect(lst_a[:]))
+        for h in range(HALVES):
+            nc.vector.tensor_copy(gb[h][:], cb_t[h][:].indirect(lst_b[:]))
+
+        hid = [pool.tile([P, R], BF16, name="hid%d" % h, align_bytes=64) for h in range(HALVES)]
+        turned = [psum.tile([P, 2, P], F32, name="turned%d" % h) for h in range(HALVES)]
+        grouped = [pool.tile([P, 4 * P], BF16, name="grouped%d" % h, align_bytes=64) for h in range(HALVES)]
+        for h in range(HALVES):
+            nc.scalar.activation(out=hid[h][:].rearrange("j (u p e) -> j u p e", u=2, e=2),
+                                 in_=acc[h][:].rearrange("j (p u e) -> j u p e", u=2, e=2), func=ACT.Relu)
+        for h in range(HALVES):
+            pairs = hid[h][:].bitcast(F32)
+            for u in range(2):
+                nc.tensor.transpose(turned[h][:, u, :], pairs[:, u * P : (u + 1) * P], ident[:])
+            nc.scalar.copy(out=grouped[h][:].bitcast(F32).rearrange("p (j u) -> p j u", u=2),
+                           in_=turned[h][:].rearrange("p u j -> p j u"))
+
+        gain = pool.tile([P, HALVES, J], F32, name="gain")
+        shift = pool.tile([P, HALVES, J], F32, name="shift")
+        for h in range(HALVES):
+            nc.scalar.activation(out=gain[:, h, :], in_=ga[h][:].bitcast(FP8), func=ACT.Copy, scale=sa_t[:, h : h + 1])
+        for h in range(HALVES):
+            nc.scalar.activation(out=shift[:, h, :], in_=gb[h][:].bitcast(FP8), func=ACT.Copy, scale=sb_t[:, h : h + 1])
+
+        hq_w = [pool.tile([P, P], U32, name="hq_w%d" % h, align_bytes=64) for h in range(HALVES)]
+        hq_s = [pool.tile([P, P], U8, name="hq_s%d" % h, align_bytes=64) for h in range(HALVES)]
+        prod = [psum.tile([P, HALVES, P], F32, name="prod%d" % h) for h in range(HALVES)]
+        for h in range(HALVES):
+            nc.vector.quantize_mx(out=hq_w[h][:].bitcast(E5M2X4), scales=hq_s[h][:], in_=grouped[h][:])
+            for m in range(HALVES):
+                ns = slice(m * P, (m + 1) * P)
+                nc.tensor.matmul_mx(out=prod[h][:, m, :], lhsT=wb_w[:, ns].bitcast(E4M3X4), lhsT_scale=wb_s[:, ns],
+                                    rhs=hq_w[h][:].bitcast(E5M2X4), rhs_scale=hq_s[h][:], start=True, stop=True)
+
+        scaled = [pool.tile([P, HALVES, P], F32, name="scaled%d" % h) for h in range(HALVES)]
+        res = [pool.tile([P, HALVES, P], F32, name="res%d" % h) for h in range(HALVES)]
+        for h in range(HALVES):
+            nc.vector.tensor_tensor(scaled[h][:], prod[h][:], gain[:, :, h * P : (h + 1) * P], ALU.mult)
+        out_rows = out.rearrange("(m p) j -> p m j", p=P)
+        for h in range(HALVES):
+            nc.vector.tensor_tensor(res[h][:], scaled[h][:], shift[:, :, h * P : (h + 1) * P], ALU.add)
+            nc.sync.dma_start(out_rows[:, :, h * P : (h + 1) * P], res[h][:])

@@ -69,32 +69,33 @@ def tile_list_gainandshift_kernel(tc, xt_words, xt_scales, xo_words, xo_scales, 
 
         nc.vector.memset(xt_s[:].bitcast(I32), 0)
         nc.vector.memset(w_s[0:64].bitcast(I32), 0)
-        nc.vector.memset(xo_s[:].bitcast(I32), 0)
         nc.vector.memset(w0_s[0:64].bitcast(I32), 0)
+        nc.vector.memset(xo_s[:].bitcast(I32), 0)
         nc.vector.memset(wb_s[:].bitcast(I32), 0)
+        nc.vector.memset(ident[:], 0.0)
 
         nc.gpsimd.dma_start(xo_w[:].bitcast(I32), words_of(xo_words))
         nc.gpsimd.dma_start(w_w[:].bitcast(I32), words_of(w_words))
-        nc.gpsimd.dma_start(w0_w[:].bitcast(I32), words_of(w0_words))
-        make_identity(nc, ident[:])
+        make_identity(nc, ident[:], nomemset=True)
 
         nc.sync.dma_start(lst_t[:], offs)
         nc.sync.dma_start(xt_w[:].bitcast(I32), xt_words[0].bitcast(I32))
         load_scale_rows(nc.sync, xt_s, xt_scales)
         load_scale_pairs(nc.sync, w_s, 0, w_scales)
         nc.sync.dma_start(lst_o[:], offs2)
-        load_scale_rows(nc.sync, xo_s, xo_scales)
         load_scale_pairs(nc.sync, w0_s, 0, w0_scales)
+        load_scale_rows(nc.sync, xo_s, xo_scales)
+        nc.sync.dma_start(w0_w[:].bitcast(I32), words_of(w0_words))
         nc.sync.dma_start(lst_a[:], offs3)
         for h in range(HALVES):
             nc.sync.dma_start(ca_t[h][:], ca[h * P : (h + 1) * P, :])
         nc.sync.dma_start(lst_b[:], offs4)
         for h in range(HALVES):
             nc.sync.dma_start(cb_t[h][:], cb[h * P : (h + 1) * P, :])
-        nc.sync.dma_start(wb_w[:].bitcast(I32), words_of(wb_words))
         with nc.allow_non_contiguous_dma(reason="one step a partition and half"):
             nc.sync.dma_start(sa_t[:], sa.rearrange("(h p) o -> p (h o)", p=P))
             nc.sync.dma_start(sb_t[:], sb.rearrange("(h p) o -> p (h o)", p=P))
+        nc.sync.dma_start(wb_w[:].bitcast(I32), words_of(wb_words))
         load_scale_rows(nc.sync, wb_s, wb_scales)
 
         gt_w = pool.tile([P, J], U16, name="gt_w", align_bytes=64)
@@ -105,10 +106,9 @@ def tile_list_gainandshift_kernel(tc, xt_words, xt_scales, xo_words, xo_scales, 
         nc.vector.tensor_copy(gt_s[:], xt_s[:].indirect(lst_t[:]))
         nc.vector.tensor_copy(w_s[64:128, 0, :].bitcast(I32), w_s[0:64, 1, :].bitcast(I32))
         nc.vector.tensor_copy(go_w[:], xo_w[:].indirect(lst_o[:]))
+        nc.vector.tensor_copy(w0_s[64:128, 0, :].bitcast(I32), w0_s[0:64, 1, :].bitcast(I32))
         for h in range(HALVES):
             nc.vector.tensor_copy(go_s[h][:], xo_s[:].indirect(lst_o[:, 8 * h : 8 * (h + 1)]))
-
-        nc.vector.tensor_copy(w0_s[64:128, 0, :].bitcast(I32), w0_s[0:64, 1, :].bitcast(I32))
 
         acc = [psum.tile([P, R], F32, name="acc%d" % h) for h in range(HALVES)]
         for h in range(HALVES):
@@ -127,7 +127,7 @@ def tile_list_gainandshift_kernel(tc, xt_words, xt_scales, xo_words, xo_scales, 
         for h in range(HALVES):
             nc.vector.tensor_copy(gb[h][:], cb_t[h][:].indirect(lst_b[:]))
 
-        hid = [pool.tile([P, R], BF16, name="hid%d" % h, align_bytes=64) for h in range(HALVES)]
+        hid = [pool.tile([P, R], BF16, name="hid%d" % h, tag="hid%d" % h, align_bytes=64) for h in range(HALVES)]
         turned = [psum.tile([P, 2, P], F32, name="turned%d" % h) for h in range(HALVES)]
         grouped = [pool.tile([P, 4 * P], BF16, name="grouped%d" % h, align_bytes=64) for h in range(HALVES)]
         for h in range(HALVES):
@@ -140,8 +140,8 @@ def tile_list_gainandshift_kernel(tc, xt_words, xt_scales, xo_words, xo_scales, 
             nc.scalar.copy(out=grouped[h][:].bitcast(F32).rearrange("p (j u) -> p j u", u=2),
                            in_=turned[h][:].rearrange("p u j -> p j u"))
 
-        gain = pool.tile([P, HALVES, J], F32, name="gain")
-        shift = pool.tile([P, HALVES, J], F32, name="shift")
+        gain = pool.tile([P, HALVES, J], F32, name="gain", tag="hid0", align_bytes=64)
+        shift = pool.tile([P, HALVES, J], F32, name="shift", tag="hid1", align_bytes=64)
         for h in range(HALVES):
             nc.scalar.activation(out=gain[:, h, :], in_=ga[h][:].bitcast(FP8), func=ACT.Copy, scale=sa_t[:, h : h + 1])
         for h in range(HALVES):

from contextlib import ExitStack

import concourse.mybir as mybir
from concourse.masks import make_identity

K, T, J, R, F, Z, V, D, N = 512, 1024, 256, 512, 512, 1024, 1024, 512, 256
FLOPS = 2 * K * R * J + 2 * F * R * J + 2 * R * N * J

F32 = mybir.dt.float32
BF16 = mybir.dt.bfloat16
I32 = mybir.dt.int32
U32 = mybir.dt.uint32
U16 = mybir.dt.uint16
U8 = mybir.dt.uint8
FP8 = mybir.dt.float8_e4m3fn
E4M3X4 = mybir.dt.float8_e4m3fn_x4
E5M2X4 = mybir.dt.float8_e5m2_x4
E2M1X4 = mybir.dt.float4_e2m1fn_x4
ACT = mybir.ActivationFunctionType
ALU = mybir.AluOpType

P = 128
HALVES = 2
QUADS = 4


def words_of(dram):
    return dram[0].rearrange("p c b -> p (c b)").bitcast(I32)


def load_scale_rows(queue, plane, scales):
    for q in range(QUADS):
        queue.dma_start(plane[32 * q : 32 * q + 4, :].bitcast(I32), scales[0, 4 * q : 4 * q + 4, :].bitcast(I32))


def load_scale_pairs(queue, staged, col, scales):
    width = scales.shape[2]
    rows = scales[0].rearrange("(s q r) c -> q r s c", s=2, q=2)
    for q in range(2):
        queue.dma_start(staged[32 * q : 32 * q + 4, :, col : col + width].bitcast(I32), rows[q].bitcast(I32))


def tile_list_gainandshift_kernel(tc, xt_words, xt_scales, xo_words, xo_scales, w_words, w_scales, w0_words, w0_scales,
                                       wb_words, wb_scales, ca, cb, sa, sb, offs, offs2, offs3, offs4, out):
    nc = tc.nc
    with ExitStack() as ctx:
        pool = ctx.enter_context(tc.tile_pool(name="held", bufs=1))
        psum = ctx.enter_context(tc.psum_pool(name="psum", bufs=1))

        lst_t = pool.tile([P, J // 16], U16, name="lst_t")
        lst_o = pool.tile([P, J // 16], U16, name="lst_o")
        lst_a = pool.tile([P, J // 16], U16, name="lst_a")
        lst_b = pool.tile([P, J // 16], U16, name="lst_b")
        xt_w = pool.tile([P, T], U16, name="xt_w", align_bytes=64)
        xt_s = pool.tile([P, T], U8, name="xt_s", align_bytes=64)
        xo_w = pool.tile([P, Z], U32, name="xo_w", align_bytes=64)
        xo_s = pool.tile([P, Z], U8, name="xo_s", align_bytes=64)
        w_w = pool.tile([P, R], U32, name="w_w", align_bytes=64)
        w0_w = pool.tile([P, R], U32, name="w0_w", align_bytes=64)
        wb_w = pool.tile([P, N], U32, name="wb_w", align_bytes=64)
        w_s = pool.tile([P, 2, R], U8, name="w_s", align_bytes=64)
        w0_s = pool.tile([P, 2, R], U8, name="w0_s", align_bytes=64)
        wb_s = pool.tile([P, N], U8, name="wb_s", align_bytes=64)
        ca_t = [pool.tile([P, V], U8, name="ca_t%d" % h) for h in range(HALVES)]
        cb_t = [pool.tile([P, D], U8, name="cb_t%d" % h) for h in range(HALVES)]
        sa_t = pool.tile([P, HALVES], F32, name="sa_t")
        sb_t = pool.tile([P, HALVES], F32, name="sb_t")
        ident = pool.tile([P, P], F32, name="ident", align_bytes=64)

        nc.vector.memset(xt_s[:].bitcast(I32), 0)
        nc.vector.memset(w_s[0:64].bitcast(I32), 0)
        nc.vector.memset(w0_s[0:64].bitcast(I32), 0)
        nc.vector.memset(xo_s[:].bitcast(I32), 0)
        nc.vector.memset(wb_s[:].bitcast(I32), 0)
        nc.vector.memset(ident[:], 0.0)

        nc.gpsimd.dma_start(xo_w[:].bitcast(I32), words_of(xo_words))
        nc.gpsimd.dma_start(w_w[:].bitcast(I32), words_of(w_words))
        make_identity(nc, ident[:], nomemset=True)

        nc.sync.dma_start(lst_t[:], offs)
        nc.sync.dma_start(xt_w[:].bitcast(I32), xt_words[0].bitcast(I32))
        load_scale_rows(nc.sync, xt_s, xt_scales)
        load_scale_pairs(nc.sync, w_s, 0, w_scales)
        nc.sync.dma_start(lst_o[:], offs2)
        load_scale_pairs(nc.sync, w0_s, 0, w0_scales)
        load_scale_rows(nc.sync, xo_s, xo_scales)
        nc.sync.dma_start(w0_w[:].bitcast(I32), words_of(w0_words))
        nc.sync.dma_start(lst_a[:], offs3)
        for h in range(HALVES):
            nc.sync.dma_start(ca_t[h][:], ca[h * P : (h + 1) * P, :])
        nc.sync.dma_start(lst_b[:], offs4)
        for h in range(HALVES):
            nc.sync.dma_start(cb_t[h][:], cb[h * P : (h + 1) * P, :])
        with nc.allow_non_contiguous_dma(reason="one step a partition and half"):
            nc.sync.dma_start(sa_t[:], sa.rearrange("(h p) o -> p (h o)", p=P))
            nc.sync.dma_start(sb_t[:], sb.rearrange("(h p) o -> p (h o)", p=P))
        nc.sync.dma_start(wb_w[:].bitcast(I32), words_of(wb_words))
        load_scale_rows(nc.sync, wb_s, wb_scales)

        gt_w = pool.tile([P, J], U16, name="gt_w", align_bytes=64)
        gt_s = pool.tile([P, J], U8, name="gt_s", align_bytes=64)
        go_w = pool.tile([P, J], U32, name="go_w", align_bytes=64)
        go_s = [pool.tile([P, P], U8, name="go_s%d" % h, align_bytes=64) for h in range(HALVES)]
        nc.vector.tensor_copy(gt_w[:], xt_w[:].indirect(lst_t[:]))
        nc.vector.tensor_copy(gt_s[:], xt_s[:].indirect(lst_t[:]))
        nc.vector.tensor_copy(w_s[64:128, 0, :].bitcast(I32), w_s[0:64, 1, :].bitcast(I32))
        nc.vector.tensor_copy(go_w[:], xo_w[:].indirect(lst_o[:]))
        nc.vector.tensor_copy(w0_s[64:128, 0, :].bitcast(I32), w0_s[0:64, 1, :].bitcast(I32))
        for h in range(HALVES):
            nc.vector.tensor_copy(go_s[h][:], xo_s[:].indirect(lst_o[:, 8 * h : 8 * (h + 1)]))

        acc = [psum.tile([P, R], F32, name="acc%d" % h) for h in range(HALVES)]
        for h in range(HALVES):
            js = slice(h * P, (h + 1) * P)
            nc.tensor.matmul_mx(out=acc[h][:], lhsT=gt_w[:, js].bitcast(E2M1X4), lhsT_scale=gt_s[:, js],
                                rhs=w_w[:].bitcast(E5M2X4), rhs_scale=w_s[:, 0, :], start=True, stop=False)
        for h in range(HALVES):
            js = slice(h * P, (h + 1) * P)
            nc.tensor.matmul_mx(out=acc[h][:], lhsT=go_w[:, js].bitcast(E5M2X4), lhsT_scale=go_s[h][:],
                                rhs=w0_w[:].bitcast(E4M3X4), rhs_scale=w0_s[:, 0, :], start=False, stop=True)

        ga = [pool.tile([P, J], U8, name="ga%d" % h) for h in range(HALVES)]
        gb = [pool.tile([P, J], U8, name="gb%d" % h) for h in range(HALVES)]
        for h in range(HALVES):
            nc.vector.tensor_copy(ga[h][:], ca_t[h][:].indirect(lst_a[:]))
        for h in range(HALVES):
            nc.vector.tensor_copy(gb[h][:], cb_t[h][:].indirect(lst_b[:]))

        hid = [pool.tile([P, R], BF16, name="hid%d" % h, tag="hid%d" % h, align_bytes=64) for h in range(HALVES)]
        turned = [psum.tile([P, 2, P], F32, name="turned%d" % h) for h in range(HALVES)]
        grouped = [pool.tile([P, 4 * P], BF16, name="grouped%d" % h, align_bytes=64) for h in range(HALVES)]
        for h in range(HALVES):
            nc.scalar.activation(out=hid[h][:].rearrange("j (u p e) -> j u p e", u=2, e=2),
                                 in_=acc[h][:].rearrange("j (p u e) -> j u p e", u=2, e=2), func=ACT.Relu)
        for h in range(HALVES):
            pairs = hid[h][:].bitcast(F32)
            for u in range(2):
                nc.tensor.transpose(turned[h][:, u, :], pairs[:, u * P : (u + 1) * P], ident[:])
            nc.scalar.copy(out=grouped[h][:].bitcast(F32).rearrange("p (j u) -> p j u", u=2),
                           in_=turned[h][:].rearrange("p u j -> p j u"))

        gain = pool.tile([P, HALVES, J], F32, name="gain", tag="hid0", align_bytes=64)
        shift = pool.tile([P, HALVES, J], F32, name="shift", tag="hid1", align_bytes=64)
        for h in range(HALVES):
            nc.scalar.activation(out=gain[:, h, :], in_=ga[h][:].bitcast(FP8), func=ACT.Copy, scale=sa_t[:, h : h + 1])
        for h in range(HALVES):
            nc.scalar.activation(out=shift[:, h, :], in_=gb[h][:].bitcast(FP8), func=ACT.Copy, scale=sb_t[:, h : h + 1])

        hq_w = [pool.tile([P, P], U32, name="hq_w%d" % h, align_bytes=64) for h in range(HALVES)]
        hq_s = [pool.tile([P, P], U8, name="hq_s%d" % h, align_bytes=64) for h in range(HALVES)]
        prod = [psum.tile([P, HALVES, P], F32, name="prod%d" % h) for h in range(HALVES)]
        for h in range(HALVES):
            nc.vector.quantize_mx(out=hq_w[h][:].bitcast(E5M2X4), scales=hq_s[h][:], in_=grouped[h][:])
            for m in range(HALVES):
                ns = slice(m * P, (m + 1) * P)
                nc.tensor.matmul_mx(out=prod[h][:, m, :], lhsT=wb_w[:, ns].bitcast(E4M3X4), lhsT_scale=wb_s[:, ns],
                                    rhs=hq_w[h][:].bitcast(E5M2X4), rhs_scale=hq_s[h][:], start=True, stop=True)

        scaled = [pool.tile([P, HALVES, P], F32, name="scaled%d" % h) for h in range(HALVES)]
        res = [pool.tile([P, HALVES, P], F32, name="res%d" % h) for h in range(HALVES)]
        for h in range(HALVES):
            nc.vector.tensor_tensor(scaled[h][:], prod[h][:], gain[:, :, h * P : (h + 1) * P], ALU.mult)
        out_rows = out.rearrange("(m p) j -> p m j", p=P)
        for h in range(HALVES):
            nc.vector.tensor_tensor(res[h][:], scaled[h][:], shift[:, :, h * P : (h + 1) * P], ALU.add)
            nc.sync.dma_start(out_rows[:, :, h * P : (h + 1) * P], res[h][:])
